import numpy as np
import ml_dtypes


def mxq(x, axis, fmt="e4m3"):
    dtype, down = {"e4m3": (ml_dtypes.float8_e4m3fn, 7), "e5m2": (ml_dtypes.float8_e5m2, 14)}[fmt]
    v = np.moveaxis(np.asarray(x, np.float32).astype(ml_dtypes.bfloat16).astype(np.float64), axis, -1)
    blocks = v.reshape(v.shape[:-1] + (-1, 32))
    amax = np.abs(blocks).max(-1, keepdims=True)
    byte = np.maximum(np.where(amax > 0, np.frexp(amax)[1] - 1 + 127, 0) - down, 1)
    scale = np.exp2(byte - 127.0)
    codes = (blocks / scale).astype(np.float32).astype(dtype).astype(np.float64)
    return np.moveaxis((codes * scale).reshape(v.shape), -1, axis)


WIDE = False


def mx_kscale(k):
    if not WIDE:
        return np.ones(k)
    levels = np.array([10, -10, 5, -5, 0])
    if k % 512:
        return np.exp2(np.random.permutation(np.resize(levels, k // 32))).repeat(32)
    a = np.empty((k // 512, 16))
    for p in range(k // 512):
        a[p, :8] = np.random.permutation(np.resize(levels, 8))
        for g in range(8):
            far = levels[np.abs(levels - a[p, g]) >= 10]
            a[p, g + 8] = far[np.random.randint(len(far))]
    return np.exp2(a.ravel()).repeat(32)


def f64(x):
    return np.asarray(x).astype(np.float64)


def striped(idx):
    return np.tile(idx.reshape(-1, 16).T, (8, 1)).astype(np.uint16)


def unstriped(offs):
    return offs[:16].T.reshape(-1).astype(np.int64)


def striped8(idx):
    return np.concatenate([x.reshape(-1, 16).T for x in idx]).astype(np.uint16)


def runs(offs, k):
    lists = np.stack([offs[16 * r : 16 * r + 16].T.reshape(-1) for r in range(8)]).astype(np.int64)
    return lists[np.arange(k) % 512 // 64]


def pack_weight(w):
    k, n = w.shape
    w = f64(np.asarray(w, np.float32).astype(ml_dtypes.bfloat16)).reshape(k // 32, 32, n)
    amax = np.abs(w).max(1)
    byte = np.clip(np.where(amax > 0, np.frexp(amax)[1] - 1 + 127 - 7, 1), 1, 254)
    scaled = (w * np.exp2(127.0 - byte)[:, None, :]).reshape(k, n).astype(np.float32)
    words = np.ascontiguousarray(scaled.reshape(k // 512, 128, 4, n).transpose(0, 1, 3, 2)).astype(ml_dtypes.float8_e4m3fn).view(np.uint8)
    return words, np.ascontiguousarray(byte.astype(np.uint8).reshape(k // 512, 16, n))


def unpack_weight(words, scales):
    g, p, n, _ = words.shape
    vals = np.ascontiguousarray(words).view(ml_dtypes.float8_e4m3fn).astype(np.float64) * np.repeat(np.exp2(scales.astype(np.float64) - 127.0), 8, axis=1)[..., None]
    return vals.transpose(0, 1, 3, 2).reshape(g * 512, n)


E2M1 = np.array([0.0, 0.5, 1.0, 1.5, 2.0, 3.0, 4.0, 6.0, -0.0, -0.5, -1.0, -1.5, -2.0, -3.0, -4.0, -6.0])


def pack_fp4(w):
    k, n = w.shape
    w = f64(np.asarray(w, np.float32).astype(ml_dtypes.bfloat16)).reshape(k // 32, 32, n)
    amax = np.abs(w).max(1)
    mant, ex = np.frexp(amax / 6.0)
    byte = np.clip(np.where(amax > 0, np.where(mant > 0.5, ex, ex - 1) + 127, 1), 1, 254)
    scaled = (w * np.exp2(127.0 - byte)[:, None, :]).reshape(k, n).astype(np.float32)
    c = np.ascontiguousarray(scaled.reshape(k // 512, 128, 4, n).transpose(0, 1, 3, 2)).astype(ml_dtypes.float4_e2m1fn).view(np.uint8) & 0xF
    words = (c[..., 0::2] | (c[..., 1::2] << 4)).reshape(k // 512, 128, 2 * n)
    return np.ascontiguousarray(words), np.ascontiguousarray(byte.astype(np.uint8).reshape(k // 512, 16, n))


def unpack_fp4(words, scales):
    g, _, n = scales.shape
    words = np.ascontiguousarray(words).reshape(g, 128, n, 2)
    nib = np.empty((g, 128, n, 4), np.uint8)
    nib[..., 0::2] = words & 0xF
    nib[..., 1::2] = words >> 4
    vals = E2M1[nib] * np.repeat(np.exp2(scales.astype(np.float64) - 127.0), 8, axis=1)[..., None]
    return vals.transpose(0, 1, 3, 2).reshape(g * 512, n)


K, T, S, N, G, H, W = 512, 2048, 256, 512, 2048, 512, 128


def setup_inputs():
    n = np.random.standard_normal
    s = mx_kscale(K)[:, None]
    u = mx_kscale(K)
    packed_xT = pack_weight(n((K, T)) * s)
    packed_dT = pack_weight(n((K, G)) / s)
    packed_w1 = pack_fp4(n((H, N)) / np.sqrt(H) / u[:, None])
    perm = np.random.permutation(S)
    return {
        "x_words": packed_xT[0],
        "x_scales": packed_xT[1],
        "d_words": packed_dT[0],
        "d_scales": packed_dT[1],
        "gn": (np.random.uniform(0.5, 1.5, (H, 1)) * u[:, None]).astype(np.float32),
        "w1_words": packed_w1[0],
        "w1_scales": packed_w1[1],
        "offs": striped8(np.random.randint(0, T, (8, S))),
        "ci": striped(np.random.permutation(G)[:H]),
        "n1": striped(perm[:W]),
        "n2": striped(perm[W:]),
        "n3": striped(np.random.permutation(S)),
    }


def reference(x_words, x_scales, d_words, d_scales, gn, w1_words, w1_scales, offs, ci, n1, n2, n3):
    d_ci = unpack_weight(d_words, d_scales)[:, unstriped(ci)]
    xq = unpack_weight(x_words, x_scales)[np.arange(K)[:, None], runs(offs, K)]
    s = 0.0625 * (d_ci.T @ xq)
    z = f64(gn) * s
    h = unpack_fp4(w1_words, w1_scales).T @ mxq(z, 0, "e4m3")
    pa = h[:, unstriped(n1)]
    pb = h[:, unstriped(n2)]
    rb = np.minimum(pa, pb)
    ra = np.maximum(pa, pb)
    ds = np.zeros((N, S))
    ds[:, unstriped(n1)] = ra
    dt = ds.copy()
    dt[:, unstriped(n2)] = rb
    return dt - dt[:, unstriped(n3)]

@@ -1,0 +1,144 @@
+from contextlib import ExitStack
+
+import concourse.mybir as mybir
+
+K, T, S, N, G, H, W = 512, 2048, 256, 512, 2048, 512, 128
+FLOPS = 2 * K * H * S + 2 * H * N * S
+
+F32 = mybir.dt.float32
+BF16 = mybir.dt.bfloat16
+I32 = mybir.dt.int32
+U32 = mybir.dt.uint32
+U16 = mybir.dt.uint16
+U8 = mybir.dt.uint8
+FP8X4 = mybir.dt.float8_e4m3fn_x4
+FP4X4 = mybir.dt.float4_e2m1fn_x4
+ALU = mybir.AluOpType
+COPY = mybir.ActivationFunctionType.Copy
+
+P = 128
+SPARE = 16
+
+
+def tile_picked_hwliordd_none_p_kernel(
+    tc, x_words, x_scales, d_words, d_scales, gn, w1_words, w1_scales, offs, ci, n1, n2, n3, out
+):
+    nc = tc.nc
+    with ExitStack() as ctx:
+        lists = ctx.enter_context(tc.tile_pool(name="lists", bufs=1))
+        keep = ctx.enter_context(tc.tile_pool(name="keep", bufs=1))
+        psum = ctx.enter_context(tc.psum_pool(name="psum", bufs=1))
+
+        offs_t = lists.tile([P, S // 16], U16)
+        ci_t = lists.tile([P, H // 16], U16)
+        n1_t = lists.tile([P, W // 16], U16)
+        n2_t = lists.tile([P, W // 16], U16)
+        n3_t = lists.tile([P, S // 16], U16)
+
+        xs_table = keep.tile([P, T], U8, align_bytes=64)
+        ds_table = keep.tile([P, G], U8, align_bytes=64)
+        xw_table = keep.tile([P, T], U32, align_bytes=64)
+        dw_table = keep.tile([P, G], U32, align_bytes=64)
+        nc.vector.memset(xs_table[:].bitcast(I32), 0)
+        nc.vector.memset(ds_table[:].bitcast(I32), 0)
+        nc.sync.dma_start(offs_t[:], offs)
+        nc.sync.dma_start(ci_t[:], ci)
+        nc.scalar.dma_start(xs_table[0:P:8, :].bitcast(I32), x_scales[0].bitcast(I32))
+        nc.scalar.dma_start(ds_table[0:P:8, :].bitcast(I32), d_scales[0].bitcast(I32))
+        nc.sync.dma_start(dw_table[:].bitcast(I32), d_words[0].rearrange("p n t -> p (n t)").bitcast(I32))
+        nc.sync.dma_start(xw_table[:].bitcast(I32), x_words[0].rearrange("p n t -> p (n t)").bitcast(I32))
+
+        gn_t = keep.tile([P, 4], F32, align_bytes=64)
+        w1w = keep.tile([P, 2 * N], U8, align_bytes=64)
+        w1s = keep.tile([P, N], U8, align_bytes=64)
+        planes = keep.tile([P, S + H], U8, align_bytes=64)
+        nc.vector.memset(planes[:].bitcast(I32), 0)
+        nc.vector.memset(w1s[:].bitcast(I32), 0)
+        nc.sync.dma_start(gn_t[:], gn.rearrange("(p t) o -> p (t o)", t=4))
+        nc.sync.dma_start(w1w[:].bitcast(I32), w1_words[0].bitcast(I32))
+        for q in range(4):
+            nc.sync.dma_start(w1s[32 * q : 32 * q + 4, :].bitcast(I32), w1_scales[0, 4 * q : 4 * q + 4, :].bitcast(I32))
+        nc.sync.dma_start(n1_t[:], n1)
+        nc.sync.dma_start(n2_t[:], n2)
+        nc.sync.dma_start(n3_t[:], n3)
+
+        dts = [keep.tile([P, S + SPARE], F32, name=f"dt{b}", align_bytes=64) for b in range(4)]
+        for b in range(4):
+            nc.vector.memset(dts[b][:], 0.0)
+
+        picked_s = keep.tile([P, S + H], U8, align_bytes=64)
+        xw = keep.tile([P, S], U32, align_bytes=64)
+        dw = keep.tile([P, H], U32, align_bytes=64)
+        nc.vector.tensor_copy(picked_s[:, 0:S], xs_table[:].indirect(offs_t[:]))
+        nc.vector.tensor_copy(
+            picked_s[:, S : S + H].rearrange("p (t m) -> p m t", t=4), ds_table[:].indirect(ci_t[:])
+        )
+        for q in range(4):
+            nc.scalar.dma_start(
+                planes[32 * q : 32 * q + 4, :].bitcast(I32), picked_s[32 * q : 32 * q + 32 : 8, :].bitcast(I32)
+            )
+        nc.vector.tensor_copy(dw[:].rearrange("p (t m) -> p m t", t=4), dw_table[:].indirect(ci_t[:]))
+        nc.vector.tensor_copy(xw[:], xw_table[:].indirect(offs_t[:]))
+
+        z_codes = keep.tile([P, S], U32, align_bytes=64)
+        z_scales = keep.tile([P, S], U8, align_bytes=64)
+        gains = gn_t[:].unsqueeze(1).to_broadcast([P, P, 4])
+        zs = []
+        for half in range(2):
+            cols = slice(P * half, P * half + P)
+            scores = psum.tile([P, 4, P], F32, name=f"scores{half}")
+            for t in range(4):
+                nc.tensor.matmul_mx(
+                    out=scores[:, t, :],
+                    lhsT=dw[:, P * t : P * t + P].bitcast(FP8X4),
+                    lhsT_scale=planes[:, S + P * t : S + P * t + P],
+                    rhs=xw[:, cols].bitcast(FP8X4),
+                    rhs_scale=planes[:, cols],
+                    start=True,
+                    stop=True,
+                )
+            z = keep.tile([P, P, 4], BF16, name=f"z{half}", align_bytes=64)
+            nc.vector.scalar_tensor_tensor(
+                z[:], scores[:].rearrange("p t n -> p n t"), 0.0625, gains, ALU.mult, ALU.mult
+            )
+            zs.append(z)
+        for half in range(2):
+            cols = slice(P * half, P * half + P)
+            nc.vector.quantize_mx(
+                out=z_codes[:, cols].bitcast(FP8X4),
+                scales=z_scales[:, cols],
+                in_=zs[half][:].rearrange("p n t -> p (n t)"),
+            )
+
+        hs = []
+        for b in range(4):
+            acc = psum.tile([P, S], F32, name=f"acc{b}")
+            nc.tensor.matmul_mx(
+                out=acc[:],
+                lhsT=w1w[:, 2 * P * b : 2 * P * (b + 1)].bitcast(FP4X4),
+                lhsT_scale=w1s[:, P * b : P * b + P],
+                rhs=z_codes[:].bitcast(FP8X4),
+                rhs_scale=z_scales[:],
+                start=True,
+                stop=True,
+            )
+            h = keep.tile([P, S], F32, name=f"h{b}", align_bytes=64)
+            nc.vector.tensor_copy(h[:], acc[:])
+            hs.append(h)
+
+        for b in range(4):
+            pa = keep.tile([P, W], F32, name=f"pa{b}", align_bytes=64)
+            pb = keep.tile([P, W], F32, name=f"pb{b}", align_bytes=64)
+            ra = keep.tile([P, W], F32, name=f"ra{b}", align_bytes=64)
+            rb = keep.tile([P, W], F32, name=f"rb{b}", align_bytes=64)
+            nc.scalar.activation(pa[:], hs[b][:].indirect(n1_t[:]), COPY)
+            nc.scalar.activation(pb[:], hs[b][:].indirect(n2_t[:]), COPY)
+            nc.vector.tensor_tensor(ra[:], pa[:], pb[:], ALU.max)
+            nc.vector.tensor_tensor(rb[:], pa[:], pb[:], ALU.min)
+            nc.scalar.activation(dts[b][:].indirect(n1_t[:]), ra[:], COPY)
+            nc.scalar.activation(dts[b][:].indirect(n2_t[:]), rb[:], COPY)
+            moved = keep.tile([P, S], F32, name=f"moved{b}", align_bytes=64)
+            nc.scalar.activation(moved[:], dts[b][:].indirect(n3_t[:]), COPY)
+            res = keep.tile([P, S], F32, name=f"res{b}", align_bytes=64)
+            nc.vector.tensor_tensor(res[:], dts[b][:, 0:S], moved[:], ALU.subtract)
+            nc.sync.dma_start(out[P * b : P * b + P, :], res[:])

@@ -35,54 +35,54 @@ def tile_picked_hwliordd_none_p_kernel(
         n2_t = lists.tile([P, W // 16], U16)
         n3_t = lists.tile([P, S // 16], U16)
 
-        xs_table = keep.tile([P, T], U8, align_bytes=64)
+        xs_table = keep.tile([P, T], U8, tag="xs_then_dw", align_bytes=64)
         ds_table = keep.tile([P, G], U8, align_bytes=64)
-        xw_table = keep.tile([P, T], U32, align_bytes=64)
-        dw_table = keep.tile([P, G], U32, align_bytes=64)
-        nc.vector.memset(xs_table[:].bitcast(I32), 0)
+        dw_table = keep.tile([P, G], U32, tag="dw_then_w1", align_bytes=64)
         nc.vector.memset(ds_table[:].bitcast(I32), 0)
+        nc.vector.memset(xs_table[:].bitcast(I32), 0)
+        gn_t = keep.tile([P, 4], F32, tag="gn_then_xw", align_bytes=64)
         nc.sync.dma_start(offs_t[:], offs)
         nc.sync.dma_start(ci_t[:], ci)
-        nc.scalar.dma_start(xs_table[0:P:8, :].bitcast(I32), x_scales[0].bitcast(I32))
+        nc.scalar.dma_start(gn_t[:], gn.rearrange("(p t) o -> p (t o)", t=4))
         nc.scalar.dma_start(ds_table[0:P:8, :].bitcast(I32), d_scales[0].bitcast(I32))
+        nc.scalar.dma_start(xs_table[0:P:8, :].bitcast(I32), x_scales[0].bitcast(I32))
         nc.sync.dma_start(dw_table[:].bitcast(I32), d_words[0].rearrange("p n t -> p (n t)").bitcast(I32))
-        nc.sync.dma_start(xw_table[:].bitcast(I32), x_words[0].rearrange("p n t -> p (n t)").bitcast(I32))
-
-        gn_t = keep.tile([P, 4], F32, align_bytes=64)
-        w1w = keep.tile([P, 2 * N], U8, align_bytes=64)
-        w1s = keep.tile([P, N], U8, align_bytes=64)
-        planes = keep.tile([P, S + H], U8, align_bytes=64)
-        nc.vector.memset(planes[:].bitcast(I32), 0)
-        nc.vector.memset(w1s[:].bitcast(I32), 0)
-        nc.sync.dma_start(gn_t[:], gn.rearrange("(p t) o -> p (t o)", t=4))
-        nc.sync.dma_start(w1w[:].bitcast(I32), w1_words[0].bitcast(I32))
-        for q in range(4):
-            nc.sync.dma_start(w1s[32 * q : 32 * q + 4, :].bitcast(I32), w1_scales[0, 4 * q : 4 * q + 4, :].bitcast(I32))
         nc.sync.dma_start(n1_t[:], n1)
         nc.sync.dma_start(n2_t[:], n2)
         nc.sync.dma_start(n3_t[:], n3)
 
+        w1s = keep.tile([P, N], U8, align_bytes=64)
+        planes = keep.tile([P, S + H], U8, align_bytes=64)
+        nc.vector.memset(w1s[:].bitcast(I32), 0)
+        nc.vector.memset(planes[:].bitcast(I32), 0)
+        for q in range(4):
+            nc.gpsimd.dma_start(w1s[32 * q : 32 * q + 4, :].bitcast(I32), w1_scales[0, 4 * q : 4 * q + 4, :].bitcast(I32))
+        gn16 = keep.tile([P, 4], F32, align_bytes=64)
+        nc.vector.tensor_scalar_mul(gn16[:], gn_t[:], 0.0625)
+        xw_table = keep.tile([P, T], U32, tag="gn_then_xw", align_bytes=64)
+        nc.sync.dma_start(xw_table[:].bitcast(I32), x_words[0].rearrange("p n t -> p (n t)").bitcast(I32))
+
         dts = [keep.tile([P, S + SPARE], F32, name=f"dt{b}", align_bytes=64) for b in range(4)]
-        for b in range(4):
-            nc.vector.memset(dts[b][:], 0.0)
 
         picked_s = keep.tile([P, S + H], U8, align_bytes=64)
         xw = keep.tile([P, S], U32, align_bytes=64)
-        dw = keep.tile([P, H], U32, align_bytes=64)
-        nc.vector.tensor_copy(picked_s[:, 0:S], xs_table[:].indirect(offs_t[:]))
         nc.vector.tensor_copy(
             picked_s[:, S : S + H].rearrange("p (t m) -> p m t", t=4), ds_table[:].indirect(ci_t[:])
         )
+        nc.vector.tensor_copy(picked_s[:, 0:S], xs_table[:].indirect(offs_t[:]))
         for q in range(4):
             nc.scalar.dma_start(
                 planes[32 * q : 32 * q + 4, :].bitcast(I32), picked_s[32 * q : 32 * q + 32 : 8, :].bitcast(I32)
             )
+        dw = keep.tile([P, H], U32, tag="xs_then_dw", align_bytes=64)
         nc.vector.tensor_copy(dw[:].rearrange("p (t m) -> p m t", t=4), dw_table[:].indirect(ci_t[:]))
+        w1w = keep.tile([P, 2 * N], U8, tag="dw_then_w1", align_bytes=64)
+        nc.sync.dma_start(w1w[:].bitcast(I32), w1_words[0].bitcast(I32))
         nc.vector.tensor_copy(xw[:], xw_table[:].indirect(offs_t[:]))
 
         z_codes = keep.tile([P, S], U32, align_bytes=64)
         z_scales = keep.tile([P, S], U8, align_bytes=64)
-        gains = gn_t[:].unsqueeze(1).to_broadcast([P, P, 4])
+        gains = gn16[:].unsqueeze(1).to_broadcast([P, P, 4])
         zs = []
         for half in range(2):
             cols = slice(P * half, P * half + P)
@@ -98,9 +98,7 @@ def tile_picked_hwliordd_none_p_kernel(
                     stop=True,
                 )
             z = keep.tile([P, P, 4], BF16, name=f"z{half}", align_bytes=64)
-            nc.vector.scalar_tensor_tensor(
-                z[:], scores[:].rearrange("p t n -> p n t"), 0.0625, gains, ALU.mult, ALU.mult
-            )
+            nc.vector.tensor_tensor(z[:], scores[:].rearrange("p t n -> p n t"), gains, ALU.mult)
             zs.append(z)
         for half in range(2):
             cols = slice(P * half, P * half + P)
@@ -112,33 +110,71 @@ def tile_picked_hwliordd_none_p_kernel(
 
         hs = []
         for b in range(4):
-            acc = psum.tile([P, S], F32, name=f"acc{b}")
-            nc.tensor.matmul_mx(
-                out=acc[:],
-                lhsT=w1w[:, 2 * P * b : 2 * P * (b + 1)].bitcast(FP4X4),
-                lhsT_scale=w1s[:, P * b : P * b + P],
-                rhs=z_codes[:].bitcast(FP8X4),
-                rhs_scale=z_scales[:],
-                start=True,
-                stop=True,
-            )
             h = keep.tile([P, S], F32, name=f"h{b}", align_bytes=64)
-            nc.vector.tensor_copy(h[:], acc[:])
+            for part, cols in enumerate([slice(0, P), slice(P, S)] if b == 0 else [slice(0, S)]):
+                acc = psum.tile([P, cols.stop - cols.start], F32, name=f"acc{b}_{part}")
+                nc.tensor.matmul_mx(
+                    out=acc[:],
+                    lhsT=w1w[:, 2 * P * b : 2 * P * (b + 1)].bitcast(FP4X4),
+                    lhsT_scale=w1s[:, P * b : P * b + P],
+                    rhs=z_codes[:, cols].bitcast(FP8X4),
+                    rhs_scale=z_scales[:, cols],
+                    start=True,
+                    stop=True,
+                )
+                if b == 0:
+                    nc.scalar.activation(h[:, cols], acc[:], COPY)
+                else:
+                    nc.vector.tensor_copy(h[:, cols], acc[:])
             hs.append(h)
 
-        for b in range(4):
-            pa = keep.tile([P, W], F32, name=f"pa{b}", align_bytes=64)
-            pb = keep.tile([P, W], F32, name=f"pb{b}", align_bytes=64)
-            ra = keep.tile([P, W], F32, name=f"ra{b}", align_bytes=64)
-            rb = keep.tile([P, W], F32, name=f"rb{b}", align_bytes=64)
-            nc.scalar.activation(pa[:], hs[b][:].indirect(n1_t[:]), COPY)
-            nc.scalar.activation(pb[:], hs[b][:].indirect(n2_t[:]), COPY)
-            nc.vector.tensor_tensor(ra[:], pa[:], pb[:], ALU.max)
-            nc.vector.tensor_tensor(rb[:], pa[:], pb[:], ALU.min)
-            nc.scalar.activation(dts[b][:].indirect(n1_t[:]), ra[:], COPY)
-            nc.scalar.activation(dts[b][:].indirect(n2_t[:]), rb[:], COPY)
-            moved = keep.tile([P, S], F32, name=f"moved{b}", align_bytes=64)
-            nc.scalar.activation(moved[:], dts[b][:].indirect(n3_t[:]), COPY)
-            res = keep.tile([P, S], F32, name=f"res{b}", align_bytes=64)
-            nc.vector.tensor_tensor(res[:], dts[b][:, 0:S], moved[:], ALU.subtract)
-            nc.sync.dma_start(out[P * b : P * b + P, :], res[:])
+        def wide(name, width):
+            return [keep.tile([P, width], F32, name=f"{name}{b}", align_bytes=64) for b in range(4)]
+
+        pa, pb, ra, rb = wide("pa", W), wide("pb", W), wide("ra", W), wide("rb", W)
+        moved, res = wide("moved", S), wide("res", S)
+
+        def fetch_first(b):
+            nc.scalar.activation(pa[b][:], hs[b][:].indirect(n1_t[:]), COPY)
+
+        def fetch_second(b):
+            nc.scalar.activation(pb[b][:], hs[b][:].indirect(n2_t[:]), COPY)
+            nc.vector.tensor_tensor(ra[b][:], pa[b][:], pb[b][:], ALU.max)
+            nc.vector.tensor_tensor(rb[b][:], pa[b][:], pb[b][:], ALU.min)
+
+        def put_larger(b):
+            nc.scalar.activation(dts[b][:].indirect(n1_t[:]), ra[b][:], COPY)
+
+        def put_smaller(b):
+            nc.scalar.activation(dts[b][:].indirect(n2_t[:]), rb[b][:], COPY)
+
+        def finish(b, cols):
+            nc.scalar.activation(
+                moved[b][:, cols], dts[b][:].indirect(n3_t[:, cols.start // 16 : cols.stop // 16]), COPY
+            )
+            nc.vector.tensor_tensor(res[b][:, cols], dts[b][:, cols], moved[b][:, cols], ALU.subtract)
+            nc.sync.dma_start(out[P * b : P * b + P, cols], res[b][:, cols])
+
+        left, right, both = slice(0, W), slice(W, S), slice(0, S)
+        fetch_first(0)
+        fetch_second(0)
+        fetch_first(1)
+        fetch_second(1)
+        put_larger(0)
+        fetch_first(2)
+        put_smaller(0)
+        fetch_second(2)
+        put_larger(1)
+        fetch_first(3)
+        put_smaller(1)
+        fetch_second(3)
+        put_larger(2)
+        finish(0, both)
+        put_smaller(2)
+        finish(1, both)
+        put_larger(3)
+        finish(2, left)
+        put_smaller(3)
+        finish(2, right)
+        finish(3, left)
+        finish(3, right)

@@ -37,30 +37,30 @@ def tile_picked_hwliordd_none_p_kernel(
 
         xs_table = keep.tile([P, T], U8, tag="xs_then_dw", align_bytes=64)
         ds_table = keep.tile([P, G], U8, align_bytes=64)
-        dw_table = keep.tile([P, G], U32, tag="dw_then_w1", align_bytes=64)
-        nc.vector.memset(ds_table[:].bitcast(I32), 0)
-        nc.vector.memset(xs_table[:].bitcast(I32), 0)
-        gn_t = keep.tile([P, 4], F32, tag="gn_then_xw", align_bytes=64)
-        nc.sync.dma_start(offs_t[:], offs)
+        dw_table = keep.tile([P, G], U32, align_bytes=64)
+        xw_table = keep.tile([P, T], U32, align_bytes=64)
+        w1w = keep.tile([P, 2 * N], U8, align_bytes=64)
+        w1s = keep.tile([P, N], U8, align_bytes=64)
+        planes = keep.tile([P, S + H], U8, align_bytes=64)
+        gn_t = keep.tile([P, 4], F32, align_bytes=64)
+        for zeroed in (xs_table, w1s, planes):
+            nc.vector.memset(zeroed[:].bitcast(I32), 0)
+
         nc.sync.dma_start(ci_t[:], ci)
-        nc.scalar.dma_start(gn_t[:], gn.rearrange("(p t) o -> p (t o)", t=4))
-        nc.scalar.dma_start(ds_table[0:P:8, :].bitcast(I32), d_scales[0].bitcast(I32))
+        nc.sync.dma_start(
+            ds_table[:].bitcast(I32), d_scales[0].bitcast(I32).unsqueeze(1).to_broadcast([16, 8, G // 4])
+        )
+        nc.sync.dma_start(offs_t[:], offs)
         nc.scalar.dma_start(xs_table[0:P:8, :].bitcast(I32), x_scales[0].bitcast(I32))
-        nc.sync.dma_start(dw_table[:].bitcast(I32), d_words[0].rearrange("p n t -> p (n t)").bitcast(I32))
         nc.sync.dma_start(n1_t[:], n1)
         nc.sync.dma_start(n2_t[:], n2)
         nc.sync.dma_start(n3_t[:], n3)
-
-        w1s = keep.tile([P, N], U8, align_bytes=64)
-        planes = keep.tile([P, S + H], U8, align_bytes=64)
-        nc.vector.memset(w1s[:].bitcast(I32), 0)
-        nc.vector.memset(planes[:].bitcast(I32), 0)
+        nc.sync.dma_start(dw_table[:].bitcast(I32), d_words[0].rearrange("p n t -> p (n t)").bitcast(I32))
+        nc.sync.dma_start(xw_table[:].bitcast(I32), x_words[0].rearrange("p n t -> p (n t)").bitcast(I32))
+        nc.sync.dma_start(w1w[:].bitcast(I32), w1_words[0].bitcast(I32))
+        nc.gpsimd.dma_start(gn_t[:], gn.rearrange("(p t) o -> p (t o)", t=4))
         for q in range(4):
             nc.gpsimd.dma_start(w1s[32 * q : 32 * q + 4, :].bitcast(I32), w1_scales[0, 4 * q : 4 * q + 4, :].bitcast(I32))
-        gn16 = keep.tile([P, 4], F32, align_bytes=64)
-        nc.vector.tensor_scalar_mul(gn16[:], gn_t[:], 0.0625)
-        xw_table = keep.tile([P, T], U32, tag="gn_then_xw", align_bytes=64)
-        nc.sync.dma_start(xw_table[:].bitcast(I32), x_words[0].rearrange("p n t -> p (n t)").bitcast(I32))
 
         dts = [keep.tile([P, S + SPARE], F32, name=f"dt{b}", align_bytes=64) for b in range(4)]
 
@@ -76,13 +76,11 @@ def tile_picked_hwliordd_none_p_kernel(
             )
         dw = keep.tile([P, H], U32, tag="xs_then_dw", align_bytes=64)
         nc.vector.tensor_copy(dw[:].rearrange("p (t m) -> p m t", t=4), dw_table[:].indirect(ci_t[:]))
-        w1w = keep.tile([P, 2 * N], U8, tag="dw_then_w1", align_bytes=64)
-        nc.sync.dma_start(w1w[:].bitcast(I32), w1_words[0].bitcast(I32))
         nc.vector.tensor_copy(xw[:], xw_table[:].indirect(offs_t[:]))
 
         z_codes = keep.tile([P, S], U32, align_bytes=64)
         z_scales = keep.tile([P, S], U8, align_bytes=64)
-        gains = gn16[:].unsqueeze(1).to_broadcast([P, P, 4])
+        gains = gn_t[:].unsqueeze(1).to_broadcast([P, P, 4])
         zs = []
         for half in range(2):
             cols = slice(P * half, P * half + P)
@@ -98,7 +96,9 @@ def tile_picked_hwliordd_none_p_kernel(
                     stop=True,
                 )
             z = keep.tile([P, P, 4], BF16, name=f"z{half}", align_bytes=64)
-            nc.vector.tensor_tensor(z[:], scores[:].rearrange("p t n -> p n t"), gains, ALU.mult)
+            nc.vector.scalar_tensor_tensor(
+                z[:], scores[:].rearrange("p t n -> p n t"), 0.0625, gains, ALU.mult, ALU.mult
+            )
             zs.append(z)
         for half in range(2):
             cols = slice(P * half, P * half + P)
@@ -176,5 +176,5 @@ def tile_picked_hwliordd_none_p_kernel(
         finish(2, left)
         put_smaller(3)
         finish(2, right)
-        finish(3, left)
-        finish(3, right)
+        finish(3, slice(0, S - 64))
+        finish(3, slice(S - 64, S))

@@ -60,22 +60,31 @@ def tile_picked_hwliordd_none_p_kernel(
         nc.sync.dma_start(w1w[:].bitcast(I32), w1_words[0].bitcast(I32))
         nc.gpsimd.dma_start(gn_t[:], gn.rearrange("(p t) o -> p (t o)", t=4))
         for q in range(4):
-            nc.gpsimd.dma_start(w1s[32 * q : 32 * q + 4, :].bitcast(I32), w1_scales[0, 4 * q : 4 * q + 4, :].bitcast(I32))
+            queue = nc.gpsimd if q < 2 else nc.sync
+            queue.dma_start(w1s[32 * q : 32 * q + 4, :].bitcast(I32), w1_scales[0, 4 * q : 4 * q + 4, :].bitcast(I32))
 
         dts = [keep.tile([P, S + SPARE], F32, name=f"dt{b}", align_bytes=64) for b in range(4)]
 
-        picked_s = keep.tile([P, S + H], U8, align_bytes=64)
+        picked_ds = keep.tile([P, H], U8, align_bytes=64)
+        picked_xs = keep.tile([P, S], U8, align_bytes=64)
+        staged = keep.tile([P, S + H], U8, align_bytes=64)
         xw = keep.tile([P, S], U32, align_bytes=64)
+        dw = keep.tile([P, H], U32, align_bytes=64)
+        nc.vector.tensor_copy(picked_ds[:], ds_table[:].indirect(ci_t[:]))
+        nc.vector.tensor_copy(picked_xs[:], xs_table[:].indirect(offs_t[:]))
         nc.vector.tensor_copy(
-            picked_s[:, S : S + H].rearrange("p (t m) -> p m t", t=4), ds_table[:].indirect(ci_t[:])
+            staged[:, S : S + H].rearrange("p (t m) -> p t m", t=4), picked_ds[:].rearrange("p (m t) -> p t m", t=4)
         )
-        nc.vector.tensor_copy(picked_s[:, 0:S], xs_table[:].indirect(offs_t[:]))
+        nc.vector.tensor_copy(staged[:, 0:S].bitcast(I32), picked_xs[:].bitcast(I32))
         for q in range(4):
             nc.scalar.dma_start(
-                planes[32 * q : 32 * q + 4, :].bitcast(I32), picked_s[32 * q : 32 * q + 32 : 8, :].bitcast(I32)
+                planes[32 * q : 32 * q + 4, :].bitcast(I32), staged[32 * q : 32 * q + 32 : 8, :].bitcast(I32)
             )
-        dw = keep.tile([P, H], U32, tag="xs_then_dw", align_bytes=64)
-        nc.vector.tensor_copy(dw[:].rearrange("p (t m) -> p m t", t=4), dw_table[:].indirect(ci_t[:]))
+        picked_dw = keep.tile([P, H], U32, tag="xs_then_dw", align_bytes=64)
+        nc.vector.tensor_copy(picked_dw[:], dw_table[:].indirect(ci_t[:]))
+        nc.vector.tensor_copy(
+            dw[:].rearrange("p (t m) -> p m t", t=4), picked_dw[:].rearrange("p (m t) -> p m t", t=4)
+        )
         nc.vector.tensor_copy(xw[:], xw_table[:].indirect(offs_t[:]))
 
         z_codes = keep.tile([P, S], U32, align_bytes=64)
@@ -155,26 +164,17 @@ def tile_picked_hwliordd_none_p_kernel(
             nc.vector.tensor_tensor(res[b][:, cols], dts[b][:, cols], moved[b][:, cols], ALU.subtract)
             nc.sync.dma_start(out[P * b : P * b + P, cols], res[b][:, cols])
 
-        left, right, both = slice(0, W), slice(W, S), slice(0, S)
-        fetch_first(0)
-        fetch_second(0)
-        fetch_first(1)
-        fetch_second(1)
-        put_larger(0)
-        fetch_first(2)
-        put_smaller(0)
-        fetch_second(2)
-        put_larger(1)
-        fetch_first(3)
-        put_smaller(1)
-        fetch_second(3)
-        put_larger(2)
-        finish(0, both)
-        put_smaller(2)
-        finish(1, both)
-        put_larger(3)
-        finish(2, left)
-        put_smaller(3)
-        finish(2, right)
+        for pair in ((0, 1), (2, 3)):
+            for b in pair:
+                fetch_first(b)
+                fetch_second(b)
+            if pair[0] > 0:
+                finish(0, slice(0, S))
+            for b in pair:
+                put_larger(b)
+            for b in pair:
+                put_smaller(b)
+        finish(1, slice(0, S))
+        finish(2, slice(0, S))
         finish(3, slice(0, S - 64))
         finish(3, slice(S - 64, S))

from contextlib import ExitStack

import concourse.mybir as mybir

K, T, S, N, G, H, W = 512, 2048, 256, 512, 2048, 512, 128
FLOPS = 2 * K * H * S + 2 * H * N * S

F32 = mybir.dt.float32
BF16 = mybir.dt.bfloat16
I32 = mybir.dt.int32
U32 = mybir.dt.uint32
U16 = mybir.dt.uint16
U8 = mybir.dt.uint8
FP8X4 = mybir.dt.float8_e4m3fn_x4
FP4X4 = mybir.dt.float4_e2m1fn_x4
ALU = mybir.AluOpType
COPY = mybir.ActivationFunctionType.Copy

P = 128
SPARE = 16


def tile_picked_hwliordd_none_p_kernel(
    tc, x_words, x_scales, d_words, d_scales, gn, w1_words, w1_scales, offs, ci, n1, n2, n3, out
):
    nc = tc.nc
    with ExitStack() as ctx:
        lists = ctx.enter_context(tc.tile_pool(name="lists", bufs=1))
        keep = ctx.enter_context(tc.tile_pool(name="keep", bufs=1))
        psum = ctx.enter_context(tc.psum_pool(name="psum", bufs=1))

        offs_t = lists.tile([P, S // 16], U16)
        ci_t = lists.tile([P, H // 16], U16)
        n1_t = lists.tile([P, W // 16], U16)
        n2_t = lists.tile([P, W // 16], U16)
        n3_t = lists.tile([P, S // 16], U16)

        xs_table = keep.tile([P, T], U8, tag="xs_then_dw", align_bytes=64)
        ds_table = keep.tile([P, G], U8, align_bytes=64)
        dw_table = keep.tile([P, G], U32, align_bytes=64)
        xw_table = keep.tile([P, T], U32, align_bytes=64)
        w1w = keep.tile([P, 2 * N], U8, align_bytes=64)
        w1s = keep.tile([P, N], U8, align_bytes=64)
        planes = keep.tile([P, S + H], U8, align_bytes=64)
        gn_t = keep.tile([P, 4], F32, align_bytes=64)
        for zeroed in (xs_table, w1s, planes):
            nc.vector.memset(zeroed[:].bitcast(I32), 0)

        nc.sync.dma_start(ci_t[:], ci)
        nc.sync.dma_start(
            ds_table[:].bitcast(I32), d_scales[0].bitcast(I32).unsqueeze(1).to_broadcast([16, 8, G // 4])
        )
        nc.sync.dma_start(offs_t[:], offs)
        nc.scalar.dma_start(xs_table[0:P:8, :].bitcast(I32), x_scales[0].bitcast(I32))
        nc.sync.dma_start(n1_t[:], n1)
        nc.sync.dma_start(n2_t[:], n2)
        nc.sync.dma_start(n3_t[:], n3)
        nc.sync.dma_start(dw_table[:].bitcast(I32), d_words[0].rearrange("p n t -> p (n t)").bitcast(I32))
        nc.sync.dma_start(xw_table[:].bitcast(I32), x_words[0].rearrange("p n t -> p (n t)").bitcast(I32))
        nc.sync.dma_start(w1w[:].bitcast(I32), w1_words[0].bitcast(I32))
        nc.gpsimd.dma_start(gn_t[:], gn.rearrange("(p t) o -> p (t o)", t=4))
        for q in range(4):
            queue = nc.gpsimd if q < 2 else nc.sync
            queue.dma_start(w1s[32 * q : 32 * q + 4, :].bitcast(I32), w1_scales[0, 4 * q : 4 * q + 4, :].bitcast(I32))

        dts = [keep.tile([P, S + SPARE], F32, name=f"dt{b}", align_bytes=64) for b in range(4)]

        picked_ds = keep.tile([P, H], U8, align_bytes=64)
        picked_xs = keep.tile([P, S], U8, align_bytes=64)
        staged = keep.tile([P, S + H], U8, align_bytes=64)
        xw = keep.tile([P, S], U32, align_bytes=64)
        dw = keep.tile([P, H], U32, align_bytes=64)
        nc.vector.tensor_copy(picked_ds[:], ds_table[:].indirect(ci_t[:]))
        nc.vector.tensor_copy(picked_xs[:], xs_table[:].indirect(offs_t[:]))
        nc.vector.tensor_copy(
            staged[:, S : S + H].rearrange("p (t m) -> p t m", t=4), picked_ds[:].rearrange("p (m t) -> p t m", t=4)
        )
        nc.vector.tensor_copy(staged[:, 0:S].bitcast(I32), picked_xs[:].bitcast(I32))
        for q in range(4):
            nc.scalar.dma_start(
                planes[32 * q : 32 * q + 4, :].bitcast(I32), staged[32 * q : 32 * q + 32 : 8, :].bitcast(I32)
            )
        picked_dw = keep.tile([P, H], U32, tag="xs_then_dw", align_bytes=64)
        nc.vector.tensor_copy(picked_dw[:], dw_table[:].indirect(ci_t[:]))
        nc.vector.tensor_copy(
            dw[:].rearrange("p (t m) -> p m t", t=4), picked_dw[:].rearrange("p (m t) -> p m t", t=4)
        )
        nc.vector.tensor_copy(xw[:], xw_table[:].indirect(offs_t[:]))

        z_codes = keep.tile([P, S], U32, align_bytes=64)
        z_scales = keep.tile([P, S], U8, align_bytes=64)
        gains = gn_t[:].unsqueeze(1).to_broadcast([P, P, 4])
        zs = []
        for half in range(2):
            cols = slice(P * half, P * half + P)
            scores = psum.tile([P, 4, P], F32, name=f"scores{half}")
            for t in range(4):
                nc.tensor.matmul_mx(
                    out=scores[:, t, :],
                    lhsT=dw[:, P * t : P * t + P].bitcast(FP8X4),
                    lhsT_scale=planes[:, S + P * t : S + P * t + P],
                    rhs=xw[:, cols].bitcast(FP8X4),
                    rhs_scale=planes[:, cols],
                    start=True,
                    stop=True,
                )
            z = keep.tile([P, P, 4], BF16, name=f"z{half}", align_bytes=64)
            nc.vector.scalar_tensor_tensor(
                z[:], scores[:].rearrange("p t n -> p n t"), 0.0625, gains, ALU.mult, ALU.mult
            )
            zs.append(z)
        for half in range(2):
            cols = slice(P * half, P * half + P)
            nc.vector.quantize_mx(
                out=z_codes[:, cols].bitcast(FP8X4),
                scales=z_scales[:, cols],
                in_=zs[half][:].rearrange("p n t -> p (n t)"),
            )

        hs = []
        for b in range(4):
            h = keep.tile([P, S], F32, name=f"h{b}", align_bytes=64)
            for part, cols in enumerate([slice(0, P), slice(P, S)] if b == 0 else [slice(0, S)]):
                acc = psum.tile([P, cols.stop - cols.start], F32, name=f"acc{b}_{part}")
                nc.tensor.matmul_mx(
                    out=acc[:],
                    lhsT=w1w[:, 2 * P * b : 2 * P * (b + 1)].bitcast(FP4X4),
                    lhsT_scale=w1s[:, P * b : P * b + P],
                    rhs=z_codes[:, cols].bitcast(FP8X4),
                    rhs_scale=z_scales[:, cols],
                    start=True,
                    stop=True,
                )
                if b == 0:
                    nc.scalar.activation(h[:, cols], acc[:], COPY)
                else:
                    nc.vector.tensor_copy(h[:, cols], acc[:])
            hs.append(h)

        def wide(name, width):
            return [keep.tile([P, width], F32, name=f"{name}{b}", align_bytes=64) for b in range(4)]

        pa, pb, ra, rb = wide("pa", W), wide("pb", W), wide("ra", W), wide("rb", W)
        moved, res = wide("moved", S), wide("res", S)

        def fetch_first(b):
            nc.scalar.activation(pa[b][:], hs[b][:].indirect(n1_t[:]), COPY)

        def fetch_second(b):
            nc.scalar.activation(pb[b][:], hs[b][:].indirect(n2_t[:]), COPY)
            nc.vector.tensor_tensor(ra[b][:], pa[b][:], pb[b][:], ALU.max)
            nc.vector.tensor_tensor(rb[b][:], pa[b][:], pb[b][:], ALU.min)

        def put_larger(b):
            nc.scalar.activation(dts[b][:].indirect(n1_t[:]), ra[b][:], COPY)

        def put_smaller(b):
            nc.scalar.activation(dts[b][:].indirect(n2_t[:]), rb[b][:], COPY)

        def finish(b, cols):
            nc.scalar.activation(
                moved[b][:, cols], dts[b][:].indirect(n3_t[:, cols.start // 16 : cols.stop // 16]), COPY
            )
            nc.vector.tensor_tensor(res[b][:, cols], dts[b][:, cols], moved[b][:, cols], ALU.subtract)
            nc.sync.dma_start(out[P * b : P * b + P, cols], res[b][:, cols])

        for pair in ((0, 1), (2, 3)):
            for b in pair:
                fetch_first(b)
                fetch_second(b)
            if pair[0] > 0:
                finish(0, slice(0, S))
            for b in pair:
                put_larger(b)
            for b in pair:
                put_smaller(b)
        finish(1, slice(0, S))
        finish(2, slice(0, S))
        finish(3, slice(0, S - 64))
        finish(3, slice(S - 64, S))
